import numpy as np
import ml_dtypes


def mxq(x, axis, fmt="e4m3"):
    dtype, down = {"e4m3": (ml_dtypes.float8_e4m3fn, 7), "e5m2": (ml_dtypes.float8_e5m2, 14)}[fmt]
    v = np.moveaxis(np.asarray(x, np.float32).astype(ml_dtypes.bfloat16).astype(np.float64), axis, -1)
    blocks = v.reshape(v.shape[:-1] + (-1, 32))
    amax = np.abs(blocks).max(-1, keepdims=True)
    byte = np.maximum(np.where(amax > 0, np.frexp(amax)[1] - 1 + 127, 0) - down, 1)
    scale = np.exp2(byte - 127.0)
    codes = (blocks / scale).astype(np.float32).astype(dtype).astype(np.float64)
    return np.moveaxis((codes * scale).reshape(v.shape), -1, axis)


WIDE = False


def mx_kscale(k):
    if not WIDE:
        return np.ones(k)
    levels = np.array([10, -10, 5, -5, 0])
    if k % 512:
        return np.exp2(np.random.permutation(np.resize(levels, k // 32))).repeat(32)
    a = np.empty((k // 512, 16))
    for p in range(k // 512):
        a[p, :8] = np.random.permutation(np.resize(levels, 8))
        for g in range(8):
            far = levels[np.abs(levels - a[p, g]) >= 10]
            a[p, g + 8] = far[np.random.randint(len(far))]
    return np.exp2(a.ravel()).repeat(32)


def f64(x):
    return np.asarray(x).astype(np.float64)


def striped(idx):
    return np.tile(idx.reshape(-1, 16).T, (8, 1)).astype(np.uint16)


def unstriped(offs):
    return offs[:16].T.reshape(-1).astype(np.int64)


E2M1 = np.array([0.0, 0.5, 1.0, 1.5, 2.0, 3.0, 4.0, 6.0, -0.0, -0.5, -1.0, -1.5, -2.0, -3.0, -4.0, -6.0])


def pack_weight(w, fmt):
    k, n = w.shape
    w = f64(np.asarray(w, np.float32).astype(ml_dtypes.bfloat16)).reshape(k // 32, 32, n)
    amax = np.abs(w).max(1)
    if fmt == "e4m3":
        byte = np.frexp(amax)[1] - 1 + 127 - 7
    else:
        mant, ex = np.frexp(amax / 6.0)
        byte = np.where(mant > 0.5, ex, ex - 1) + 127
    byte = np.clip(np.where(amax > 0, byte, 1), 1, 254)
    scaled = (w * np.exp2(127.0 - byte)[:, None, :]).reshape(k, n).astype(np.float32)
    by_word = np.ascontiguousarray(scaled.reshape(k // 512, 128, 4, n).transpose(0, 1, 3, 2))
    if fmt == "e4m3":
        words = by_word.astype(ml_dtypes.float8_e4m3fn).view(np.uint8)
    else:
        c = by_word.astype(ml_dtypes.float4_e2m1fn).view(np.uint8) & 0xF
        words = (c[..., 0::2] | (c[..., 1::2] << 4)).reshape(k // 512, 128, 2 * n)
    return np.ascontiguousarray(words), np.ascontiguousarray(byte.astype(np.uint8).reshape(k // 512, 16, n))


def unpack_weight(words, scales, fmt):
    g, _, n = scales.shape
    words = np.ascontiguousarray(words).reshape(g, 128, n, -1)
    if fmt == "e4m3":
        vals = words.view(ml_dtypes.float8_e4m3fn).astype(np.float64)
    else:
        nib = np.empty((g, 128, n, 4), np.uint8)
        nib[..., 0::2] = words & 0xF
        nib[..., 1::2] = words >> 4
        vals = E2M1[nib]
    vals = vals * np.repeat(np.exp2(scales.astype(np.float64) - 127.0), 8, axis=1)[..., None]
    return vals.transpose(0, 1, 3, 2).reshape(g * 512, n)


def gelu(v):
    return 0.5 * v * (1.0 + np.tanh(np.sqrt(2.0 / np.pi) * (v + 0.044715 * v**3)))


K, T, S, H, T2, P, N = 1536, 2048, 1024, 1024, 2048, 1024, 384

def setup_inputs():
    n = np.random.standard_normal
    s = mx_kscale(K)[:, None]
    u = mx_kscale(H)[:, None]
    d = {}
    d["tab_words"], d["tab_scales"] = pack_weight(n((K, T)) * s, "e4m3")
    d["offs"] = striped(np.random.permutation(T)[:S])
    d["w1"] = (n((K, H)) / s * u.T / K**0.5).astype(np.float32)
    d["base"] = (n((H, S)) * u).astype(np.float32)
    d["page0"] = (n((H, T2)) * u).astype(np.float32)
    d["wgs"] = np.exp(0.3 * n((128, S))).astype(np.float32)
    d["offs2"] = striped(np.random.permutation(T2)[:S])
    d["offs3"] = striped(np.random.permutation(T2)[:P])
    d["gain"] = np.exp(0.4 * n(H)).astype(np.float32)
    d["w2_words"], d["w2_scales"] = pack_weight(1.2 * n((H, N)) / u / H**0.5, "e2m1")
    d["w3"] = (1.2 * n((H, N)) / u / H**0.5).astype(np.float32)
    d["page1"] = (1.5 * n((N, T2))).astype(np.float32)
    d["wgo"] = np.exp(0.3 * n((128, P))).astype(np.float32)
    d["offs4"] = striped(np.random.permutation(T2)[:P])
    return d

def reference(tab_words, tab_scales, offs, w1, base, page0, wgs, offs2, offs3, gain, w2_words, w2_scales, w3, page1, wgo, offs4):
    v = unpack_weight(tab_words, tab_scales, "e4m3")[:, unstriped(offs)]
    h = np.maximum(mxq(f64(w1), 0, "e4m3").T @ v, f64(base))
    page = f64(page0).copy()
    page[:, unstriped(offs2)] = np.tile(f64(wgs), (H // 128, 1)) * h
    x = mxq(f64(gain)[:, None] * page[:, unstriped(offs3)], 0, "e4m3")
    y2 = unpack_weight(w2_words, w2_scales, "e2m1").T @ x
    y3 = mxq(f64(w3), 0, "e4m3").T @ x
    y = np.sqrt(np.square(y2) + np.square(y3) + 1.0)
    out = f64(page1).copy()
    out[:, unstriped(offs4)] = np.tile(f64(wgo), (N // 128, 1)) * y
    return out

@@ -1,0 +1,349 @@
+from contextlib import ExitStack
+
+import concourse.mybir as mybir
+from concourse.masks import make_identity
+
+K, T, S, H, N = 1536, 2048, 1024, 1024, 384
+FLOPS = 2 * K * H * S + 2 * 2 * H * N * S
+
+F32 = mybir.dt.float32
+BF16 = mybir.dt.bfloat16
+I32 = mybir.dt.int32
+U32 = mybir.dt.uint32
+U16 = mybir.dt.uint16
+U8 = mybir.dt.uint8
+FP8X4 = mybir.dt.float8_e4m3fn_x4
+FP4X4 = mybir.dt.float4_e2m1fn_x4
+ACT = mybir.ActivationFunctionType
+MULT = mybir.AluOpType.mult
+MAX = mybir.AluOpType.max
+
+P = 128
+PACK = 4
+KP = P * PACK
+BANK = 512
+QW = 256
+QUARTERS = S // QW
+WHOLE = ((0, PACK),)
+HALVES = ((0, PACK // 2), (PACK // 2, PACK))
+
+
+def tile_list_folio_legibility_page_kernel(
+    tc, tab_words, tab_scales, offs, w1, base, page0, wgs, offs2, offs3, gain, w2_words, w2_scales, w3, page1, wgo, offs4, out
+):
+    nc = tc.nc
+    k_passes = K // KP
+    r_passes = H // KP
+    n_tiles = N // P
+
+    with ExitStack() as ctx:
+        lists = ctx.enter_context(tc.tile_pool(name="lists", bufs=1))
+        sb = ctx.enter_context(tc.tile_pool(name="sb", bufs=1))
+        psum = ctx.enter_context(tc.psum_pool(name="psum", bufs=1))
+
+        def sbuf(name, shape, dtype, tag=None, bufs=1):
+            return sb.tile(shape, dtype, name=name, tag=tag or name, bufs=bufs, align_bytes=64)
+
+        def bank(name, index, width):
+            return psum.tile([P, width], F32, name=name, tag="bank%d" % index)
+
+        def load_list(name, src):
+            tile = lists.tile([P, S // 16], U16, name=name)
+            nc.sync.dma_start(tile[:], src)
+            return tile
+
+        def entries(lst, j0, j1):
+            return lst[:, j0 // 16 : j1 // 16]
+
+        warm = sbuf("warm", [P, 1], F32)
+        nc.vector.memset(warm[:], 1.0)
+        warm_out = sbuf("warm_out", [P, 1], F32)
+        nc.scalar.activation(warm_out[:], warm[:], ACT.Sqrt)
+
+        tab_s = sbuf("tab_s", [P, T], U8)
+        nc.vector.memset(tab_s[:].bitcast(I32), 0)
+        w2_s = sbuf("w2_s", [P, r_passes, N], U8)
+        nc.gpsimd.memset(w2_s[:].rearrange("p a c -> p (a c)").bitcast(I32), 0)
+        ident = sbuf("ident", [P, P], F32)
+        make_identity(nc, ident[:])
+
+        idx = load_list("idx", offs)
+
+        def gather_table(a):
+            window = sbuf("tab_w%d" % a, [P, T], I32, tag="wide%d" % a)
+            nc.sync.dma_start(window[:], tab_words[a].rearrange("p t i -> p (t i)").bitcast(I32))
+            picked = sbuf("v_w%d" % a, [P, S], U32)
+            nc.vector.tensor_copy(picked[:], window[:].bitcast(U32).indirect(idx[:]))
+            return picked
+
+        def round_w1(a, b, parts):
+            raw = sbuf("w1_raw%d%d" % (a, b), [P, PACK, KP], F32, tag="raw%d" % a)
+            rows = w1[KP * a : KP * (a + 1), KP * b : KP * (b + 1)]
+            nc.sync.dma_start(raw[:], rows.rearrange("(p i) c -> p i c", i=PACK))
+            woven = sbuf("w1_bf%d%d" % (a, b), [P, PACK * KP], BF16, tag="bf%d" % a)
+            for t0, t1 in parts:
+                nc.scalar.copy(
+                    woven[:, KP * t0 : KP * t1].rearrange("p (t m i) -> p m t i", m=P, i=PACK),
+                    raw[:].rearrange("p i (m t) -> p m t i", t=PACK)[:, :, t0:t1, :],
+                )
+            return woven
+
+        def quantize_w1(a, b, woven, codes, parts):
+            scales = sbuf("w1_s%d%d" % (a, b), [P, KP], U8)
+            for t0, t1 in parts:
+                nc.vector.quantize_mx(
+                    out=codes[:, P * t0 : P * t1].bitcast(FP8X4),
+                    scales=scales[:, P * t0 : P * t1],
+                    in_=woven[:, KP * t0 : KP * t1],
+                )
+            w1_q[a, b] = (codes, scales)
+
+        def first_w1(a):
+            codes = sbuf("w1_c%d" % a, [P, KP], U32)
+            parts = HALVES if a == k_passes - 1 else WHOLE
+            quantize_w1(a, 0, round_w1(a, 0, parts), codes[:], parts)
+
+        def round_w3(a):
+            raw = sbuf("w3_raw%d" % a, [P, PACK, N], F32, tag="raw%d" % a)
+            nc.sync.dma_start(raw[:], w3[KP * a : KP * (a + 1), :].rearrange("(p i) c -> p i c", i=PACK))
+            woven = sbuf("w3_bf%d" % a, [P, PACK * N], BF16, tag="bf%d" % a)
+            nc.scalar.copy(woven[:].rearrange("p (c i) -> p c i", i=PACK), raw[:].rearrange("p i c -> p c i"))
+            return woven
+
+        def quantize_w3(a, woven, codes):
+            scales = sbuf("w3_s%d" % a, [P, N], U8)
+            for c0, c1 in ((0, 256), (256, N)):
+                nc.vector.quantize_mx(
+                    out=codes[:, c0:c1].bitcast(FP8X4), scales=scales[:, c0:c1], in_=woven[:, PACK * c0 : PACK * c1]
+                )
+            return codes, scales
+
+        v_w = [None] * k_passes
+        w1_q = {}
+        v_w[0] = gather_table(0)
+        for quad in range(4):
+            nc.sync.dma_start(
+                tab_s[32 * quad : 32 * quad + 4 * k_passes, :].bitcast(I32),
+                tab_scales[:, 4 * quad : 4 * quad + 4, :].bitcast(I32),
+            )
+        v_s = sbuf("v_s", [P, S], U8)
+        nc.vector.tensor_copy(v_s[:], tab_s[:].indirect(idx[:]))
+        v_w[1] = gather_table(1)
+        first_w1(0)
+        v_w[2] = gather_table(2)
+        first_w1(1)
+        first_w1(2)
+
+        wgs_rows = wgs.rearrange("(q t) j -> q t j", t=PACK)
+        wgs_first = sbuf("wgs_first", [P, 1, S], F32, tag="wgs_first")
+        wgs_rest = sbuf("wgs_rest", [P, PACK - 1, S], F32, tag="wgs_rest")
+
+        def load_wgs(tile, t0, t1):
+            for g in range(4):
+                nc.sync.dma_start(tile[32 * g : 32 * (g + 1), :, :], wgs_rows[:, t0:t1, :])
+
+        def slice_rows(src, b, t):
+            return src[KP * b : KP * (b + 1), :].rearrange("(p t) j -> t p j", t=PACK)[t]
+
+        pages = {}
+        held = {}
+
+        def make_features(i):
+            b, t = divmod(i, PACK)
+            floor = sbuf("base%d" % i, [P, S], F32, tag="row%d" % (i % 3))
+            nc.sync.dma_start(floor[:], slice_rows(base, b, t))
+            if i == 0:
+                load_wgs(wgs_first, 0, 1)
+                held["idx2"] = load_list("idx2", offs2)
+            if i == 1:
+                load_wgs(wgs_rest, 1, PACK)
+            page = sbuf("page%d" % i, [P, T], F32)
+            nc.sync.dma_start(page[:], slice_rows(page0, b, t))
+            pages[b, t] = page
+            h = sbuf("h%d" % i, [P, S], F32, tag="h", bufs=2)
+            for half in range(S // BANK):
+                cols = slice(BANK * half, BANK * (half + 1))
+                acc = bank("h_acc%d%d" % (i, half), 2 * (i % 2) + half, BANK)
+                for a in range(k_passes):
+                    codes, scales = w1_q[a, b]
+                    nc.tensor.matmul_mx(
+                        out=acc[:],
+                        lhsT=codes[:, P * t : P * (t + 1)].bitcast(FP8X4),
+                        lhsT_scale=scales[:, P * t : P * (t + 1)],
+                        rhs=v_w[a][:, cols].bitcast(FP8X4),
+                        rhs_scale=v_s[4 * a : P, cols],
+                        start=(a == 0),
+                        stop=(a == k_passes - 1),
+                    )
+                nc.vector.tensor_tensor(h[:, cols], acc[:], floor[:, cols], MAX)
+            return h
+
+        def put_features(i, h):
+            b, t = divmod(i, PACK)
+            factor = wgs_first[:, 0, :] if t == 0 else wgs_rest[:, t - 1, :]
+            nc.vector.tensor_tensor(pages[b, t][:].indirect(held["idx2"][:]), h[:], factor, MULT)
+
+        def recall(b, t, dst, j0, j1):
+            nc.vector.tensor_copy(dst, pages[b, t][:].indirect(entries(held["idx3"], j0, j1)))
+
+        def weave(b, t, woven, src):
+            nc.scalar.activation(
+                woven.rearrange("p (j t) -> p t j", t=PACK)[:, t, :],
+                src,
+                ACT.Copy,
+                scale=held["gain"][:, b, t : t + 1],
+            )
+
+        x_q = {}
+
+        def quantize_x(b, q, codes, woven):
+            scales = sbuf("x_s%d%d" % (b, q), [P, QW], U8)
+            nc.vector.quantize_mx(out=codes.bitcast(FP8X4), scales=scales[:], in_=woven)
+            x_q[b, q] = (codes, scales)
+
+        early = QUARTERS - 1
+        tiles = r_passes * PACK
+        x_bf0 = sbuf("x_bf0", [P, PACK * S], BF16)
+        h = make_features(0)
+        held["idx3"] = load_list("idx3", offs3)
+        held["gain"] = sbuf("gain_sb", [P, r_passes, PACK], F32)
+        nc.sync.dma_start(held["gain"][:], gain.rearrange("(a p t) -> p a t", p=P, t=PACK))
+        for i in range(tiles):
+            b, t = divmod(i, PACK)
+            put_features(i, h)
+            if i == PACK:
+                first = sbuf("x_c00", [P, QW], U32, tag="wgs_first")
+                quantize_x(0, 0, first[:], x_bf0[:, 0 : PACK * QW])
+            if i + 1 < tiles:
+                h = make_features(i + 1)
+            got = sbuf("got%d" % i, [P, S], F32, tag="row%d" % ((i + 1) % 3))
+            if b == 0:
+                recall(0, t, got[:], 0, S)
+                weave(0, t, x_bf0[:], got[:])
+            else:
+                if t < PACK - 1:
+                    recall(1, t, got[:, 0 : early * QW], 0, early * QW)
+                for q in range(early):
+                    cols = slice(QW * q, QW * (q + 1))
+                    if t == PACK - 1:
+                        recall(1, t, got[:, cols], cols.start, cols.stop)
+                    weave(1, t, x_bf1[q][:], got[:, cols])
+            if i == 0:
+                w1_bf = [round_w1(a, 1, WHOLE) for a in range(k_passes)]
+            if i == 2:
+                codes = sbuf("w1_c1", [P, k_passes * KP], U32, tag="page2")
+                for a in range(k_passes):
+                    quantize_w1(a, 1, w1_bf[a], codes[:, KP * a : KP * (a + 1)], WHOLE)
+                w3_bf = [round_w3(a) for a in range(r_passes)]
+                x_bf1 = [sbuf("x_bf1%d" % q, [P, PACK * QW], BF16, tag="raw%d" % q) for q in range(early)]
+            if i == 3:
+                codes = sbuf("w3_c", [P, r_passes * N], U32, tag="page3")
+                w3_q = [quantize_w3(a, w3_bf[a], codes[:, N * a : N * (a + 1)]) for a in range(r_passes)]
+                w2_w = sbuf("w2_w", [P, r_passes, 2 * N], U8)
+                nc.sync.dma_start(w2_w[:].bitcast(I32), w2_words.rearrange("a p c -> p a c").bitcast(I32))
+                for quad in range(4):
+                    nc.sync.dma_start(
+                        w2_s[32 * quad : 32 * quad + 4, :, :].bitcast(I32),
+                        w2_scales[:, 4 * quad : 4 * quad + 4, :].rearrange("a r c -> r a c").bitcast(I32),
+                    )
+            if i == 4:
+                idx4 = load_list("idx4", offs4)
+                wgo_sb = sbuf("wgo_sb", [P, S], F32)
+                nc.sync.dma_start(wgo_sb[:], wgo)
+                legible = []
+                for n in range(n_tiles):
+                    tile = sbuf("legible%d" % n, [P, T], F32, tag="wide%d" % n)
+                    nc.sync.dma_start(tile[:], page1[P * n : P * (n + 1), :])
+                    legible.append(tile)
+
+        x_c0 = sbuf("x_c0", [P, early, QW], U32, tag="wgs_rest")
+
+        def quantize_quarter(b, q):
+            if b == 0:
+                quantize_x(0, q, x_c0[:, q - 1, :], x_bf0[:, PACK * QW * q : PACK * QW * (q + 1)])
+            else:
+                codes = sbuf("x_c1%d" % q, [P, QW], U32)
+                quantize_x(1, q, codes[:], x_bf1[q][:])
+
+        quantize_quarter(1, 0)
+        quantize_quarter(0, 1)
+        quantize_quarter(1, 1)
+        late = sbuf("late", [P, PACK, QW], F32, tag="raw0")
+        for t in range(PACK):
+            recall(1, t, late[:, t, :], early * QW, S)
+        quantize_quarter(0, 2)
+        quantize_quarter(1, 2)
+        quantize_quarter(0, 3)
+
+        square_tag = ["bf0", "bf1", "bf2", "bf0", "bf1", "bf2", "bf1", "bf2"]
+        y_last = sbuf("y_last", [P, 2 * QW], F32)
+
+        def score(q):
+            accs = {}
+            for jt in range(2):
+                accs[jt] = (bank("y2_%d%d" % (q, jt), 2 * jt, N), bank("y3_%d%d" % (q, jt), 2 * jt + 1, N))
+            for b in range(r_passes):
+                codes, scales = x_q[b, q]
+                for jt in range(2):
+                    lhs = codes[:, P * jt : P * (jt + 1)].bitcast(FP8X4)
+                    lhs_scale = scales[:, P * jt : P * (jt + 1)]
+                    for n in range(n_tiles):
+                        nc.tensor.matmul_mx(
+                            out=accs[jt][0][:, P * n : P * (n + 1)],
+                            lhsT=lhs,
+                            lhsT_scale=lhs_scale,
+                            rhs=w2_w[:, b, 2 * P * n : 2 * P * (n + 1)].bitcast(FP4X4),
+                            rhs_scale=w2_s[:, b, P * n : P * (n + 1)],
+                            start=(b == 0 and n == 0),
+                            stop=(b == r_passes - 1 and n == n_tiles - 1),
+                        )
+                    for c0, c1 in ((0, 256), (256, N)):
+                        nc.tensor.matmul_mx(
+                            out=accs[jt][1][:, c0:c1],
+                            lhsT=lhs,
+                            lhsT_scale=lhs_scale,
+                            rhs=w3_q[b][0][:, c0:c1].bitcast(FP8X4),
+                            rhs_scale=w3_q[b][1][:, c0:c1],
+                            start=(b == 0 and c0 == 0),
+                            stop=(b == r_passes - 1 and c1 == N),
+                        )
+            sums = [bank("sum%d%d" % (q, n), 4 + (n_tiles * q + n) % 4, QW) for n in range(n_tiles)]
+            for jt in range(2):
+                squares = sbuf("sq%d%d" % (q, jt), [P, 2, N], F32, tag=square_tag[2 * q + jt])
+                for which in range(2):
+                    nc.scalar.activation(squares[:, which, :], accs[jt][which][:], ACT.Square)
+                for n in range(n_tiles):
+                    for which in range(2):
+                        nc.tensor.matmul(
+                            sums[n][:, P * jt : P * (jt + 1)],
+                            squares[:, which, P * n : P * (n + 1)],
+                            ident[:],
+                            start=(which == 0),
+                            stop=(which == 1),
+                            is_transpose=True,
+                        )
+            for n in range(n_tiles):
+                j0, j1 = QW * q, QW * (q + 1)
+                joined = n == n_tiles - 1 and q >= QUARTERS - 2
+                if joined:
+                    y = y_last[:, QW * (q - 2) : QW * (q - 1)]
+                else:
+                    y_tile = sbuf("y%d%d" % (q, n), [P, QW], F32, tag="y", bufs=6)
+                    y = y_tile[:]
+                nc.scalar.activation(y, sums[n][:], ACT.Sqrt, bias=1.0)
+                if joined:
+                    if q == QUARTERS - 2:
+                        continue
+                    y, j0 = y_last[:], j0 - QW
+                nc.vector.tensor_tensor(legible[n][:].indirect(entries(idx4, j0, j1)), y, wgo_sb[:, j0:j1], MULT)
+                if q == QUARTERS - 1:
+                    nc.sync.dma_start(out[P * n : P * (n + 1), :], legible[n][:])
+
+        score(0)
+        score(1)
+        x_bf1.append(sbuf("x_bf13", [P, PACK * QW], BF16, tag="bf0"))
+        for t in range(PACK):
+            weave(1, t, x_bf1[early][:], late[:, t, :])
+        quantize_quarter(1, early)
+        score(2)
+        score(3)

@@ -24,8 +24,6 @@ KP = P * PACK
 BANK = 512
 QW = 256
 QUARTERS = S // QW
-WHOLE = ((0, PACK),)
-HALVES = ((0, PACK // 2), (PACK // 2, PACK))
 
 
 def tile_list_folio_legibility_page_kernel(
@@ -69,39 +67,35 @@ def tile_list_folio_legibility_page_kernel(
 
         idx = load_list("idx", offs)
 
-        def gather_table(a):
+        def gather_table(a, parts):
             window = sbuf("tab_w%d" % a, [P, T], I32, tag="wide%d" % a)
             nc.sync.dma_start(window[:], tab_words[a].rearrange("p t i -> p (t i)").bitcast(I32))
             picked = sbuf("v_w%d" % a, [P, S], U32)
-            nc.vector.tensor_copy(picked[:], window[:].bitcast(U32).indirect(idx[:]))
+            for j0 in range(0, S, S // parts):
+                j1 = j0 + S // parts
+                nc.vector.tensor_copy(picked[:, j0:j1], window[:].bitcast(U32).indirect(entries(idx, j0, j1)))
             return picked
 
-        def round_w1(a, b, parts):
-            raw = sbuf("w1_raw%d%d" % (a, b), [P, PACK, KP], F32, tag="raw%d" % a)
-            rows = w1[KP * a : KP * (a + 1), KP * b : KP * (b + 1)]
-            nc.sync.dma_start(raw[:], rows.rearrange("(p i) c -> p i c", i=PACK))
-            woven = sbuf("w1_bf%d%d" % (a, b), [P, PACK * KP], BF16, tag="bf%d" % a)
-            for t0, t1 in parts:
-                nc.scalar.copy(
-                    woven[:, KP * t0 : KP * t1].rearrange("p (t m i) -> p m t i", m=P, i=PACK),
-                    raw[:].rearrange("p i (m t) -> p m t i", t=PACK)[:, :, t0:t1, :],
-                )
-            return woven
+        def load_w1(a, c0, c1):
+            raw = sbuf("w1_raw%d_%d" % (a, c0), [P, PACK, c1 - c0], F32, tag="raw%d" % a)
+            nc.sync.dma_start(raw[:], w1[KP * a : KP * (a + 1), c0:c1].rearrange("(p i) c -> p i c", i=PACK))
+            return raw
 
-        def quantize_w1(a, b, woven, codes, parts):
-            scales = sbuf("w1_s%d%d" % (a, b), [P, KP], U8)
-            for t0, t1 in parts:
-                nc.vector.quantize_mx(
-                    out=codes[:, P * t0 : P * t1].bitcast(FP8X4),
-                    scales=scales[:, P * t0 : P * t1],
-                    in_=woven[:, KP * t0 : KP * t1],
-                )
-            w1_q[a, b] = (codes, scales)
+        def interleave(woven, planes):
+            nc.scalar.copy(woven.rearrange("p (c i) -> p c i", i=PACK), planes.rearrange("p i c -> p c i"))
 
-        def first_w1(a):
-            codes = sbuf("w1_c%d" % a, [P, KP], U32)
-            parts = HALVES if a == k_passes - 1 else WHOLE
-            quantize_w1(a, 0, round_w1(a, 0, parts), codes[:], parts)
+        def quantize(woven, codes, scales):
+            nc.vector.quantize_mx(out=codes.bitcast(FP8X4), scales=scales, in_=woven)
+
+        w1_q = {}
+        w1_s = sbuf("w1_s", [P, k_passes * H], U8)
+
+        def quantize_w1(a, i0, i1, woven, codes):
+            scales = w1_s[:, H * a + P * i0 : H * a + P * i1]
+            quantize(woven, codes, scales)
+            for i in range(i0, i1):
+                cols = slice(P * (i - i0), P * (i - i0 + 1))
+                w1_q[a, i] = (codes[:, cols], scales[:, cols])
 
         def round_w3(a):
             raw = sbuf("w3_raw%d" % a, [P, PACK, N], F32, tag="raw%d" % a)
@@ -119,8 +113,7 @@ def tile_list_folio_legibility_page_kernel(
             return codes, scales
 
         v_w = [None] * k_passes
-        w1_q = {}
-        v_w[0] = gather_table(0)
+        v_w[0] = gather_table(0, 1)
         for quad in range(4):
             nc.sync.dma_start(
                 tab_s[32 * quad : 32 * quad + 4 * k_passes, :].bitcast(I32),
@@ -128,48 +121,51 @@ def tile_list_folio_legibility_page_kernel(
             )
         v_s = sbuf("v_s", [P, S], U8)
         nc.vector.tensor_copy(v_s[:], tab_s[:].indirect(idx[:]))
-        v_w[1] = gather_table(1)
-        first_w1(0)
-        v_w[2] = gather_table(2)
-        first_w1(1)
-        first_w1(2)
+        v_w[1] = gather_table(1, 1)
+        for a in range(k_passes):
+            woven = sbuf("w1_bf%d_0" % a, [P, KP], BF16, tag="bf%d" % a)
+            interleave(woven[:], load_w1(a, 0, P)[:])
+            codes = sbuf("w1_c%d_0" % a, [P, P], U32)
+            quantize_w1(a, 0, 1, woven[:], codes[:])
+        v_w[2] = gather_table(2, 2)
 
-        wgs_rows = wgs.rearrange("(q t) j -> q t j", t=PACK)
-        wgs_first = sbuf("wgs_first", [P, 1, S], F32, tag="wgs_first")
-        wgs_rest = sbuf("wgs_rest", [P, PACK - 1, S], F32, tag="wgs_rest")
+        wgs_plain = sbuf("wgs_plain", [P, S], F32)
+        wgs_dealt = [sbuf("wgs_dealt%d" % u, [P, 2, S], F32) for u in range(2)]
 
-        def load_wgs(tile, t0, t1):
-            for g in range(4):
-                nc.sync.dma_start(tile[32 * g : 32 * (g + 1), :, :], wgs_rows[:, t0:t1, :])
-
-        def slice_rows(src, b, t):
-            return src[KP * b : KP * (b + 1), :].rearrange("(p t) j -> t p j", t=PACK)[t]
+        def tile_rows(src, i):
+            if i < PACK:
+                return src[P * i : P * (i + 1), :]
+            return src[KP:, :].rearrange("(p t) j -> t p j", t=PACK)[i - PACK]
 
         pages = {}
         held = {}
 
         def make_features(i):
-            b, t = divmod(i, PACK)
             floor = sbuf("base%d" % i, [P, S], F32, tag="row%d" % (i % 3))
-            nc.sync.dma_start(floor[:], slice_rows(base, b, t))
+            nc.sync.dma_start(floor[:], tile_rows(base, i))
             if i == 0:
-                load_wgs(wgs_first, 0, 1)
+                nc.sync.dma_start(wgs_plain[:], wgs)
                 held["idx2"] = load_list("idx2", offs2)
-            if i == 1:
-                load_wgs(wgs_rest, 1, PACK)
+            if i in (PACK, PACK + 2):
+                u = (i - PACK) // 2
+                for g in range(4):
+                    nc.sync.dma_start(
+                        wgs_dealt[u][32 * g : 32 * (g + 1), :, :],
+                        wgs.rearrange("(q t) j -> q t j", t=PACK)[:, 2 * u : 2 * u + 2, :],
+                    )
             page = sbuf("page%d" % i, [P, T], F32)
-            nc.sync.dma_start(page[:], slice_rows(page0, b, t))
-            pages[b, t] = page
+            nc.sync.dma_start(page[:], tile_rows(page0, i))
+            pages[i] = page
             h = sbuf("h%d" % i, [P, S], F32, tag="h", bufs=2)
             for half in range(S // BANK):
                 cols = slice(BANK * half, BANK * (half + 1))
                 acc = bank("h_acc%d%d" % (i, half), 2 * (i % 2) + half, BANK)
                 for a in range(k_passes):
-                    codes, scales = w1_q[a, b]
+                    codes, scales = w1_q[a, i]
                     nc.tensor.matmul_mx(
                         out=acc[:],
-                        lhsT=codes[:, P * t : P * (t + 1)].bitcast(FP8X4),
-                        lhsT_scale=scales[:, P * t : P * (t + 1)],
+                        lhsT=codes.bitcast(FP8X4),
+                        lhsT_scale=scales,
                         rhs=v_w[a][:, cols].bitcast(FP8X4),
                         rhs_scale=v_s[4 * a : P, cols],
                         start=(a == 0),
@@ -179,19 +175,18 @@ def tile_list_folio_legibility_page_kernel(
             return h
 
         def put_features(i, h):
-            b, t = divmod(i, PACK)
-            factor = wgs_first[:, 0, :] if t == 0 else wgs_rest[:, t - 1, :]
-            nc.vector.tensor_tensor(pages[b, t][:].indirect(held["idx2"][:]), h[:], factor, MULT)
+            factor = wgs_plain[:] if i < PACK else wgs_dealt[(i - PACK) // 2][:, i % 2, :]
+            nc.vector.tensor_tensor(pages[i][:].indirect(held["idx2"][:]), h[:], factor, MULT)
 
         def recall(b, t, dst, j0, j1):
-            nc.vector.tensor_copy(dst, pages[b, t][:].indirect(entries(held["idx3"], j0, j1)))
+            nc.vector.tensor_copy(dst, pages[PACK * b + t][:].indirect(entries(held["idx3"], j0, j1)))
 
         def weave(b, t, woven, src):
             nc.scalar.activation(
                 woven.rearrange("p (j t) -> p t j", t=PACK)[:, t, :],
                 src,
                 ACT.Copy,
-                scale=held["gain"][:, b, t : t + 1],
+                scale=held["gain_dealt"][:, t : t + 1],
             )
 
         x_q = {}
@@ -203,23 +198,49 @@ def tile_list_folio_legibility_page_kernel(
 
         early = QUARTERS - 1
         tiles = r_passes * PACK
+        x_planes = sbuf("x_planes", [P, PACK, S], BF16)
         x_bf0 = sbuf("x_bf0", [P, PACK * S], BF16)
         h = make_features(0)
+        raws = [load_w1(a, P, KP) for a in range(k_passes)]
         held["idx3"] = load_list("idx3", offs3)
-        held["gain"] = sbuf("gain_sb", [P, r_passes, PACK], F32)
-        nc.sync.dma_start(held["gain"][:], gain.rearrange("(a p t) -> p a t", p=P, t=PACK))
+        gain_plain = sbuf("gain_plain", [P, PACK], F32)
+        with nc.allow_non_contiguous_dma(reason="one gain for each partition"):
+            nc.sync.dma_start(gain_plain[:], gain[0:KP].rearrange("(c p) -> p c", p=P))
+        held["gain_dealt"] = sbuf("gain_dealt", [P, PACK], F32)
+        nc.sync.dma_start(held["gain_dealt"][:], gain[KP:].rearrange("(p t) -> p t", t=PACK))
+        second = sbuf("w1_bf_1", [P, k_passes * KP], BF16, tag="second")
+        others = [sbuf("w1_bf%d_2" % a, [P, 2 * KP], BF16, tag="bf%d" % a) for a in range(k_passes)]
+        for a in range(k_passes):
+            interleave(second[:, KP * a : KP * (a + 1)], raws[a][:, :, 0:P])
+        for a in range(k_passes):
+            interleave(others[a][:], raws[a][:, :, P:])
         for i in range(tiles):
             b, t = divmod(i, PACK)
             put_features(i, h)
-            if i == PACK:
-                first = sbuf("x_c00", [P, QW], U32, tag="wgs_first")
+            if i == 0:
+                codes = sbuf("w1_c_1", [P, k_passes * P], U32)
+                for a in range(k_passes):
+                    quantize_w1(a, 1, 2, second[:, KP * a : KP * (a + 1)], codes[:, P * a : P * (a + 1)])
+                got = sbuf("got0", [P, S], F32, tag="second")
+                recall(0, 0, got[:], 0, S)
+            if i == PACK + 1:
+                first = sbuf("x_c00", [P, QW], U32, tag="wgs_dealt0")
                 quantize_x(0, 0, first[:], x_bf0[:, 0 : PACK * QW])
             if i + 1 < tiles:
                 h = make_features(i + 1)
-            got = sbuf("got%d" % i, [P, S], F32, tag="row%d" % ((i + 1) % 3))
+            if i == 0:
+                codes = sbuf("w1_c_2", [P, k_passes * 2 * P], U32, tag="row1")
+                for a in range(k_passes):
+                    quantize_w1(a, 2, PACK, others[a][:], codes[:, 2 * P * a : 2 * P * (a + 1)])
+            else:
+                got = sbuf("got%d" % i, [P, S], F32, tag="row%d" % ((i + 1) % 3))
             if b == 0:
-                recall(0, t, got[:], 0, S)
-                weave(0, t, x_bf0[:], got[:])
+                if i > 0:
+                    recall(0, t, got[:], 0, S)
+                scaled = sbuf("scaled%d" % i, [P, S], BF16, tag="scaled", bufs=2)
+                nc.scalar.activation(scaled[:], got[:], ACT.Copy, scale=gain_plain[:, i : i + 1])
+                for plane in range(PACK):
+                    nc.sync.dma_start(x_planes[32 * i : 32 * (i + 1), plane, :], scaled[plane:P:PACK, :])
             else:
                 if t < PACK - 1:
                     recall(1, t, got[:, 0 : early * QW], 0, early * QW)
@@ -228,14 +249,25 @@ def tile_list_folio_legibility_page_kernel(
                     if t == PACK - 1:
                         recall(1, t, got[:, cols], cols.start, cols.stop)
                     weave(1, t, x_bf1[q][:], got[:, cols])
-            if i == 0:
-                w1_bf = [round_w1(a, 1, WHOLE) for a in range(k_passes)]
+            if i == 1:
+                w1_bf = []
+                for a in range(k_passes):
+                    raw = load_w1(a, KP, H)
+                    woven = sbuf("w1_bf%d_4" % a, [P, PACK * KP], BF16, tag="bf%d" % a)
+                    nc.scalar.copy(
+                        woven[:].rearrange("p (t m i) -> p m t i", t=PACK, i=PACK),
+                        raw[:].rearrange("p i (m t) -> p m t i", t=PACK),
+                    )
+                    w1_bf.append(woven)
             if i == 2:
                 codes = sbuf("w1_c1", [P, k_passes * KP], U32, tag="page2")
                 for a in range(k_passes):
-                    quantize_w1(a, 1, w1_bf[a], codes[:, KP * a : KP * (a + 1)], WHOLE)
+                    quantize_w1(a, PACK, tiles, w1_bf[a][:], codes[:, KP * a : KP * (a + 1)])
                 w3_bf = [round_w3(a) for a in range(r_passes)]
                 x_bf1 = [sbuf("x_bf1%d" % q, [P, PACK * QW], BF16, tag="raw%d" % q) for q in range(early)]
+            if i == 3:
+                for q in range(QUARTERS):
+                    interleave(x_bf0[:, PACK * QW * q : PACK * QW * (q + 1)], x_planes[:, :, QW * q : QW * (q + 1)])
             if i == 3:
                 codes = sbuf("w3_c", [P, r_passes * N], U32, tag="page3")
                 w3_q = [quantize_w3(a, w3_bf[a], codes[:, N * a : N * (a + 1)]) for a in range(r_passes)]
@@ -256,7 +288,7 @@ def tile_list_folio_legibility_page_kernel(
                     nc.sync.dma_start(tile[:], page1[P * n : P * (n + 1), :])
                     legible.append(tile)
 
-        x_c0 = sbuf("x_c0", [P, early, QW], U32, tag="wgs_rest")
+        x_c0 = sbuf("x_c0", [P, early, QW], U32, tag="wgs_dealt1")
 
         def quantize_quarter(b, q):
             if b == 0:

@@ -59,7 +59,7 @@ def tile_list_folio_legibility_page_kernel(
         nc.scalar.activation(warm_out[:], warm[:], ACT.Sqrt)
 
         tab_s = sbuf("tab_s", [P, T], U8)
-        nc.vector.memset(tab_s[:].bitcast(I32), 0)
+        nc.gpsimd.memset(tab_s[:].bitcast(I32), 0)
         w2_s = sbuf("w2_s", [P, r_passes, N], U8)
         nc.gpsimd.memset(w2_s[:].rearrange("p a c -> p (a c)").bitcast(I32), 0)
         ident = sbuf("ident", [P, P], F32)
@@ -76,10 +76,10 @@ def tile_list_folio_legibility_page_kernel(
                 nc.vector.tensor_copy(picked[:, j0:j1], window[:].bitcast(U32).indirect(entries(idx, j0, j1)))
             return picked
 
-        def load_w1(a, c0, c1):
-            raw = sbuf("w1_raw%d_%d" % (a, c0), [P, PACK, c1 - c0], F32, tag="raw%d" % a)
-            nc.sync.dma_start(raw[:], w1[KP * a : KP * (a + 1), c0:c1].rearrange("(p i) c -> p i c", i=PACK))
-            return raw
+        def load_w1(a, raw, c0, c1):
+            planes = raw[:, PACK * (c0 % KP) : PACK * (c0 % KP + c1 - c0)].rearrange("p (i c) -> p i c", i=PACK)
+            nc.sync.dma_start(planes, w1[KP * a : KP * (a + 1), c0:c1].rearrange("(p i) c -> p i c", i=PACK))
+            return planes
 
         def interleave(woven, planes):
             nc.scalar.copy(woven.rearrange("p (c i) -> p c i", i=PACK), planes.rearrange("p i c -> p c i"))
@@ -122,9 +122,10 @@ def tile_list_folio_legibility_page_kernel(
         v_s = sbuf("v_s", [P, S], U8)
         nc.vector.tensor_copy(v_s[:], tab_s[:].indirect(idx[:]))
         v_w[1] = gather_table(1, 1)
+        raws = [sbuf("w1_raw%d" % a, [P, PACK * KP], F32, tag="raw%d" % a) for a in range(k_passes)]
         for a in range(k_passes):
             woven = sbuf("w1_bf%d_0" % a, [P, KP], BF16, tag="bf%d" % a)
-            interleave(woven[:], load_w1(a, 0, P)[:])
+            interleave(woven[:], load_w1(a, raws[a], 0, P))
             codes = sbuf("w1_c%d_0" % a, [P, P], U32)
             quantize_w1(a, 0, 1, woven[:], codes[:])
         v_w[2] = gather_table(2, 2)
@@ -140,12 +141,34 @@ def tile_list_folio_legibility_page_kernel(
         pages = {}
         held = {}
 
+        def load_floor(i, half):
+            floor = sbuf("base%d%d" % (i, half), [P, BANK], F32, tag="%s%d" % (("row", "half")[half], i % 3))
+            nc.sync.dma_start(floor[:], tile_rows(base, i)[:, BANK * half : BANK * (half + 1)])
+            return floor
+
+        def load_page(i):
+            page = sbuf("page%d" % i, [P, T], F32)
+            nc.sync.dma_start(page[:], tile_rows(page0, i))
+            pages[i] = page
+
+        def features(i, half, floor, h):
+            cols = slice(BANK * half, BANK * (half + 1))
+            acc = bank("h_acc%d%d" % (i, half), 2 * (i % 2) + half, BANK)
+            for a in range(k_passes):
+                codes, scales = w1_q[a, i]
+                nc.tensor.matmul_mx(
+                    out=acc[:],
+                    lhsT=codes.bitcast(FP8X4),
+                    lhsT_scale=scales,
+                    rhs=v_w[a][:, cols].bitcast(FP8X4),
+                    rhs_scale=v_s[4 * a : P, cols],
+                    start=(a == 0),
+                    stop=(a == k_passes - 1),
+                )
+            nc.vector.tensor_tensor(h[:, cols], acc[:], floor[:], MAX)
+
         def make_features(i):
-            floor = sbuf("base%d" % i, [P, S], F32, tag="row%d" % (i % 3))
-            nc.sync.dma_start(floor[:], tile_rows(base, i))
-            if i == 0:
-                nc.sync.dma_start(wgs_plain[:], wgs)
-                held["idx2"] = load_list("idx2", offs2)
+            floors = [load_floor(i, half) for half in range(2)]
             if i in (PACK, PACK + 2):
                 u = (i - PACK) // 2
                 for g in range(4):
@@ -153,30 +176,15 @@ def tile_list_folio_legibility_page_kernel(
                         wgs_dealt[u][32 * g : 32 * (g + 1), :, :],
                         wgs.rearrange("(q t) j -> q t j", t=PACK)[:, 2 * u : 2 * u + 2, :],
                     )
-            page = sbuf("page%d" % i, [P, T], F32)
-            nc.sync.dma_start(page[:], tile_rows(page0, i))
-            pages[i] = page
+            load_page(i)
             h = sbuf("h%d" % i, [P, S], F32, tag="h", bufs=2)
-            for half in range(S // BANK):
-                cols = slice(BANK * half, BANK * (half + 1))
-                acc = bank("h_acc%d%d" % (i, half), 2 * (i % 2) + half, BANK)
-                for a in range(k_passes):
-                    codes, scales = w1_q[a, i]
-                    nc.tensor.matmul_mx(
-                        out=acc[:],
-                        lhsT=codes.bitcast(FP8X4),
-                        lhsT_scale=scales,
-                        rhs=v_w[a][:, cols].bitcast(FP8X4),
-                        rhs_scale=v_s[4 * a : P, cols],
-                        start=(a == 0),
-                        stop=(a == k_passes - 1),
-                    )
-                nc.vector.tensor_tensor(h[:, cols], acc[:], floor[:, cols], MAX)
+            for half in range(2):
+                features(i, half, floors[half], h)
             return h
 
-        def put_features(i, h):
+        def put_features(i, h, j0, j1):
             factor = wgs_plain[:] if i < PACK else wgs_dealt[(i - PACK) // 2][:, i % 2, :]
-            nc.vector.tensor_tensor(pages[i][:].indirect(held["idx2"][:]), h[:], factor, MULT)
+            nc.vector.tensor_tensor(pages[i][:].indirect(entries(held["idx2"], j0, j1)), h[:, j0:j1], factor[:, j0:j1], MULT)
 
         def recall(b, t, dst, j0, j1):
             nc.vector.tensor_copy(dst, pages[PACK * b + t][:].indirect(entries(held["idx3"], j0, j1)))
@@ -198,25 +206,30 @@ def tile_list_folio_legibility_page_kernel(
 
         early = QUARTERS - 1
         tiles = r_passes * PACK
+        scaled = []
         x_planes = sbuf("x_planes", [P, PACK, S], BF16)
         x_bf0 = sbuf("x_bf0", [P, PACK * S], BF16)
-        h = make_features(0)
-        raws = [load_w1(a, P, KP) for a in range(k_passes)]
-        held["idx3"] = load_list("idx3", offs3)
-        gain_plain = sbuf("gain_plain", [P, PACK], F32)
-        with nc.allow_non_contiguous_dma(reason="one gain for each partition"):
-            nc.sync.dma_start(gain_plain[:], gain[0:KP].rearrange("(c p) -> p c", p=P))
-        held["gain_dealt"] = sbuf("gain_dealt", [P, PACK], F32)
-        nc.sync.dma_start(held["gain_dealt"][:], gain[KP:].rearrange("(p t) -> p t", t=PACK))
+        h = sbuf("h0", [P, S], F32, tag="h", bufs=2)
+        for half in range(2):
+            cols = slice(BANK * half, BANK * (half + 1))
+            floor = load_floor(0, half)
+            nc.sync.dma_start(wgs_plain[:, cols], wgs[:, cols])
+            if half == 0:
+                held["idx2"] = load_list("idx2", offs2)
+                load_page(0)
+            features(0, half, floor, h)
+            put_features(0, h, cols.start, cols.stop)
         second = sbuf("w1_bf_1", [P, k_passes * KP], BF16, tag="second")
         others = [sbuf("w1_bf%d_2" % a, [P, 2 * KP], BF16, tag="bf%d" % a) for a in range(k_passes)]
         for a in range(k_passes):
-            interleave(second[:, KP * a : KP * (a + 1)], raws[a][:, :, 0:P])
+            interleave(second[:, KP * a : KP * (a + 1)], load_w1(a, raws[a], P, 2 * P))
+        held["idx3"] = load_list("idx3", offs3)
         for a in range(k_passes):
-            interleave(others[a][:], raws[a][:, :, P:])
+            interleave(others[a][:], load_w1(a, raws[a], 2 * P, KP))
         for i in range(tiles):
             b, t = divmod(i, PACK)
-            put_features(i, h)
+            if i > 0:
+                put_features(i, h, 0, S)
             if i == 0:
                 codes = sbuf("w1_c_1", [P, k_passes * P], U32)
                 for a in range(k_passes):
@@ -229,6 +242,11 @@ def tile_list_folio_legibility_page_kernel(
             if i + 1 < tiles:
                 h = make_features(i + 1)
             if i == 0:
+                gain_plain = sbuf("gain_plain", [P, PACK], F32)
+                with nc.allow_non_contiguous_dma(reason="one gain for each partition"):
+                    nc.sync.dma_start(gain_plain[:], gain[0:KP].rearrange("(c p) -> p c", p=P))
+                held["gain_dealt"] = sbuf("gain_dealt", [P, PACK], F32)
+                nc.sync.dma_start(held["gain_dealt"][:], gain[KP:].rearrange("(p t) -> p t", t=PACK))
                 codes = sbuf("w1_c_2", [P, k_passes * 2 * P], U32, tag="row1")
                 for a in range(k_passes):
                     quantize_w1(a, 2, PACK, others[a][:], codes[:, 2 * P * a : 2 * P * (a + 1)])
@@ -237,10 +255,9 @@ def tile_list_folio_legibility_page_kernel(
             if b == 0:
                 if i > 0:
                     recall(0, t, got[:], 0, S)
-                scaled = sbuf("scaled%d" % i, [P, S], BF16, tag="scaled", bufs=2)
-                nc.scalar.activation(scaled[:], got[:], ACT.Copy, scale=gain_plain[:, i : i + 1])
-                for plane in range(PACK):
-                    nc.sync.dma_start(x_planes[32 * i : 32 * (i + 1), plane, :], scaled[plane:P:PACK, :])
+                rows = sbuf("scaled%d" % i, [P, S], BF16, tag=("scaled", "second", "page0", "page1")[i])
+                nc.scalar.activation(rows[:], got[:], ACT.Copy, scale=gain_plain[:, i : i + 1])
+                scaled.append(rows)
             else:
                 if t < PACK - 1:
                     recall(1, t, got[:, 0 : early * QW], 0, early * QW)
@@ -252,11 +269,12 @@ def tile_list_folio_legibility_page_kernel(
             if i == 1:
                 w1_bf = []
                 for a in range(k_passes):
-                    raw = load_w1(a, KP, H)
+                    raw = sbuf("w1_raw%d_4" % a, [P, PACK * KP], F32, tag="raw%d" % a)
+                    planes = load_w1(a, raw, KP, H)
                     woven = sbuf("w1_bf%d_4" % a, [P, PACK * KP], BF16, tag="bf%d" % a)
                     nc.scalar.copy(
                         woven[:].rearrange("p (t m i) -> p m t i", t=PACK, i=PACK),
-                        raw[:].rearrange("p i (m t) -> p m t i", t=PACK),
+                        planes.rearrange("p i (m t) -> p m t i", t=PACK),
                     )
                     w1_bf.append(woven)
             if i == 2:
@@ -265,9 +283,6 @@ def tile_list_folio_legibility_page_kernel(
                     quantize_w1(a, PACK, tiles, w1_bf[a][:], codes[:, KP * a : KP * (a + 1)])
                 w3_bf = [round_w3(a) for a in range(r_passes)]
                 x_bf1 = [sbuf("x_bf1%d" % q, [P, PACK * QW], BF16, tag="raw%d" % q) for q in range(early)]
-            if i == 3:
-                for q in range(QUARTERS):
-                    interleave(x_bf0[:, PACK * QW * q : PACK * QW * (q + 1)], x_planes[:, :, QW * q : QW * (q + 1)])
             if i == 3:
                 codes = sbuf("w3_c", [P, r_passes * N], U32, tag="page3")
                 w3_q = [quantize_w3(a, w3_bf[a], codes[:, N * a : N * (a + 1)]) for a in range(r_passes)]
@@ -287,6 +302,11 @@ def tile_list_folio_legibility_page_kernel(
                     tile = sbuf("legible%d" % n, [P, T], F32, tag="wide%d" % n)
                     nc.sync.dma_start(tile[:], page1[P * n : P * (n + 1), :])
                     legible.append(tile)
+                for c in range(PACK):
+                    for plane in range(PACK):
+                        nc.sync.dma_start(x_planes[32 * c : 32 * (c + 1), plane, :], scaled[c][plane:P:PACK, :])
+                for q in range(QUARTERS):
+                    interleave(x_bf0[:, PACK * QW * q : PACK * QW * (q + 1)], x_planes[:, :, QW * q : QW * (q + 1)])
 
         x_c0 = sbuf("x_c0", [P, early, QW], U32, tag="wgs_dealt1")
 
@@ -360,7 +380,7 @@ def tile_list_folio_legibility_page_kernel(
                 if joined:
                     y = y_last[:, QW * (q - 2) : QW * (q - 1)]
                 else:
-                    y_tile = sbuf("y%d%d" % (q, n), [P, QW], F32, tag="y", bufs=6)
+                    y_tile = sbuf("y%d%d" % (q, n), [P, QW], F32, tag="y", bufs=4)
                     y = y_tile[:]
                 nc.scalar.activation(y, sums[n][:], ACT.Sqrt, bias=1.0)
                 if joined:
@@ -374,8 +394,10 @@ def tile_list_folio_legibility_page_kernel(
         score(0)
         score(1)
         x_bf1.append(sbuf("x_bf13", [P, PACK * QW], BF16, tag="bf0"))
+        late_bf = sbuf("late_bf", [P, PACK, QW], BF16, tag="scaled")
         for t in range(PACK):
-            weave(1, t, x_bf1[early][:], late[:, t, :])
+            nc.scalar.activation(late_bf[:, t, :], late[:, t, :], ACT.Copy, scale=held["gain_dealt"][:, t : t + 1])
+        interleave(x_bf1[early][:], late_bf[:])
         quantize_quarter(1, early)
         score(2)
         score(3)

from contextlib import ExitStack

import concourse.mybir as mybir
from concourse.masks import make_identity

K, T, S, H, N = 1536, 2048, 1024, 1024, 384
FLOPS = 2 * K * H * S + 2 * 2 * H * N * S

F32 = mybir.dt.float32
BF16 = mybir.dt.bfloat16
I32 = mybir.dt.int32
U32 = mybir.dt.uint32
U16 = mybir.dt.uint16
U8 = mybir.dt.uint8
FP8X4 = mybir.dt.float8_e4m3fn_x4
FP4X4 = mybir.dt.float4_e2m1fn_x4
ACT = mybir.ActivationFunctionType
MULT = mybir.AluOpType.mult
MAX = mybir.AluOpType.max

P = 128
PACK = 4
KP = P * PACK
BANK = 512
QW = 256
QUARTERS = S // QW


def tile_list_folio_legibility_page_kernel(
    tc, tab_words, tab_scales, offs, w1, base, page0, wgs, offs2, offs3, gain, w2_words, w2_scales, w3, page1, wgo, offs4, out
):
    nc = tc.nc
    k_passes = K // KP
    r_passes = H // KP
    n_tiles = N // P

    with ExitStack() as ctx:
        lists = ctx.enter_context(tc.tile_pool(name="lists", bufs=1))
        sb = ctx.enter_context(tc.tile_pool(name="sb", bufs=1))
        psum = ctx.enter_context(tc.psum_pool(name="psum", bufs=1))

        def sbuf(name, shape, dtype, tag=None, bufs=1):
            return sb.tile(shape, dtype, name=name, tag=tag or name, bufs=bufs, align_bytes=64)

        def bank(name, index, width):
            return psum.tile([P, width], F32, name=name, tag="bank%d" % index)

        def load_list(name, src):
            tile = lists.tile([P, S // 16], U16, name=name)
            nc.sync.dma_start(tile[:], src)
            return tile

        def entries(lst, j0, j1):
            return lst[:, j0 // 16 : j1 // 16]

        warm = sbuf("warm", [P, 1], F32)
        nc.vector.memset(warm[:], 1.0)
        warm_out = sbuf("warm_out", [P, 1], F32)
        nc.scalar.activation(warm_out[:], warm[:], ACT.Sqrt)

        tab_s = sbuf("tab_s", [P, T], U8)
        nc.gpsimd.memset(tab_s[:].bitcast(I32), 0)
        w2_s = sbuf("w2_s", [P, r_passes, N], U8)
        nc.gpsimd.memset(w2_s[:].rearrange("p a c -> p (a c)").bitcast(I32), 0)
        ident = sbuf("ident", [P, P], F32)
        make_identity(nc, ident[:])

        idx = load_list("idx", offs)

        def gather_table(a, parts):
            window = sbuf("tab_w%d" % a, [P, T], I32, tag="wide%d" % a)
            nc.sync.dma_start(window[:], tab_words[a].rearrange("p t i -> p (t i)").bitcast(I32))
            picked = sbuf("v_w%d" % a, [P, S], U32)
            for j0 in range(0, S, S // parts):
                j1 = j0 + S // parts
                nc.vector.tensor_copy(picked[:, j0:j1], window[:].bitcast(U32).indirect(entries(idx, j0, j1)))
            return picked

        def load_w1(a, raw, c0, c1):
            planes = raw[:, PACK * (c0 % KP) : PACK * (c0 % KP + c1 - c0)].rearrange("p (i c) -> p i c", i=PACK)
            nc.sync.dma_start(planes, w1[KP * a : KP * (a + 1), c0:c1].rearrange("(p i) c -> p i c", i=PACK))
            return planes

        def interleave(woven, planes):
            nc.scalar.copy(woven.rearrange("p (c i) -> p c i", i=PACK), planes.rearrange("p i c -> p c i"))

        def quantize(woven, codes, scales):
            nc.vector.quantize_mx(out=codes.bitcast(FP8X4), scales=scales, in_=woven)

        w1_q = {}
        w1_s = sbuf("w1_s", [P, k_passes * H], U8)

        def quantize_w1(a, i0, i1, woven, codes):
            scales = w1_s[:, H * a + P * i0 : H * a + P * i1]
            quantize(woven, codes, scales)
            for i in range(i0, i1):
                cols = slice(P * (i - i0), P * (i - i0 + 1))
                w1_q[a, i] = (codes[:, cols], scales[:, cols])

        def round_w3(a):
            raw = sbuf("w3_raw%d" % a, [P, PACK, N], F32, tag="raw%d" % a)
            nc.sync.dma_start(raw[:], w3[KP * a : KP * (a + 1), :].rearrange("(p i) c -> p i c", i=PACK))
            woven = sbuf("w3_bf%d" % a, [P, PACK * N], BF16, tag="bf%d" % a)
            nc.scalar.copy(woven[:].rearrange("p (c i) -> p c i", i=PACK), raw[:].rearrange("p i c -> p c i"))
            return woven

        def quantize_w3(a, woven, codes):
            scales = sbuf("w3_s%d" % a, [P, N], U8)
            for c0, c1 in ((0, 256), (256, N)):
                nc.vector.quantize_mx(
                    out=codes[:, c0:c1].bitcast(FP8X4), scales=scales[:, c0:c1], in_=woven[:, PACK * c0 : PACK * c1]
                )
            return codes, scales

        v_w = [None] * k_passes
        v_w[0] = gather_table(0, 1)
        for quad in range(4):
            nc.sync.dma_start(
                tab_s[32 * quad : 32 * quad + 4 * k_passes, :].bitcast(I32),
                tab_scales[:, 4 * quad : 4 * quad + 4, :].bitcast(I32),
            )
        v_s = sbuf("v_s", [P, S], U8)
        nc.vector.tensor_copy(v_s[:], tab_s[:].indirect(idx[:]))
        v_w[1] = gather_table(1, 1)
        raws = [sbuf("w1_raw%d" % a, [P, PACK * KP], F32, tag="raw%d" % a) for a in range(k_passes)]
        for a in range(k_passes):
            woven = sbuf("w1_bf%d_0" % a, [P, KP], BF16, tag="bf%d" % a)
            interleave(woven[:], load_w1(a, raws[a], 0, P))
            codes = sbuf("w1_c%d_0" % a, [P, P], U32)
            quantize_w1(a, 0, 1, woven[:], codes[:])
        v_w[2] = gather_table(2, 2)

        wgs_plain = sbuf("wgs_plain", [P, S], F32)
        wgs_dealt = [sbuf("wgs_dealt%d" % u, [P, 2, S], F32) for u in range(2)]

        def tile_rows(src, i):
            if i < PACK:
                return src[P * i : P * (i + 1), :]
            return src[KP:, :].rearrange("(p t) j -> t p j", t=PACK)[i - PACK]

        pages = {}
        held = {}

        def load_floor(i, half):
            floor = sbuf("base%d%d" % (i, half), [P, BANK], F32, tag="%s%d" % (("row", "half")[half], i % 3))
            nc.sync.dma_start(floor[:], tile_rows(base, i)[:, BANK * half : BANK * (half + 1)])
            return floor

        def load_page(i):
            page = sbuf("page%d" % i, [P, T], F32)
            nc.sync.dma_start(page[:], tile_rows(page0, i))
            pages[i] = page

        def features(i, half, floor, h):
            cols = slice(BANK * half, BANK * (half + 1))
            acc = bank("h_acc%d%d" % (i, half), 2 * (i % 2) + half, BANK)
            for a in range(k_passes):
                codes, scales = w1_q[a, i]
                nc.tensor.matmul_mx(
                    out=acc[:],
                    lhsT=codes.bitcast(FP8X4),
                    lhsT_scale=scales,
                    rhs=v_w[a][:, cols].bitcast(FP8X4),
                    rhs_scale=v_s[4 * a : P, cols],
                    start=(a == 0),
                    stop=(a == k_passes - 1),
                )
            nc.vector.tensor_tensor(h[:, cols], acc[:], floor[:], MAX)

        def make_features(i):
            floors = [load_floor(i, half) for half in range(2)]
            if i in (PACK, PACK + 2):
                u = (i - PACK) // 2
                for g in range(4):
                    nc.sync.dma_start(
                        wgs_dealt[u][32 * g : 32 * (g + 1), :, :],
                        wgs.rearrange("(q t) j -> q t j", t=PACK)[:, 2 * u : 2 * u + 2, :],
                    )
            load_page(i)
            h = sbuf("h%d" % i, [P, S], F32, tag="h", bufs=2)
            for half in range(2):
                features(i, half, floors[half], h)
            return h

        def put_features(i, h, j0, j1):
            factor = wgs_plain[:] if i < PACK else wgs_dealt[(i - PACK) // 2][:, i % 2, :]
            nc.vector.tensor_tensor(pages[i][:].indirect(entries(held["idx2"], j0, j1)), h[:, j0:j1], factor[:, j0:j1], MULT)

        def recall(b, t, dst, j0, j1):
            nc.vector.tensor_copy(dst, pages[PACK * b + t][:].indirect(entries(held["idx3"], j0, j1)))

        def weave(b, t, woven, src):
            nc.scalar.activation(
                woven.rearrange("p (j t) -> p t j", t=PACK)[:, t, :],
                src,
                ACT.Copy,
                scale=held["gain_dealt"][:, t : t + 1],
            )

        x_q = {}

        def quantize_x(b, q, codes, woven):
            scales = sbuf("x_s%d%d" % (b, q), [P, QW], U8)
            nc.vector.quantize_mx(out=codes.bitcast(FP8X4), scales=scales[:], in_=woven)
            x_q[b, q] = (codes, scales)

        early = QUARTERS - 1
        tiles = r_passes * PACK
        scaled = []
        x_planes = sbuf("x_planes", [P, PACK, S], BF16)
        x_bf0 = sbuf("x_bf0", [P, PACK * S], BF16)
        h = sbuf("h0", [P, S], F32, tag="h", bufs=2)
        for half in range(2):
            cols = slice(BANK * half, BANK * (half + 1))
            floor = load_floor(0, half)
            nc.sync.dma_start(wgs_plain[:, cols], wgs[:, cols])
            if half == 0:
                held["idx2"] = load_list("idx2", offs2)
                load_page(0)
            features(0, half, floor, h)
            put_features(0, h, cols.start, cols.stop)
        second = sbuf("w1_bf_1", [P, k_passes * KP], BF16, tag="second")
        others = [sbuf("w1_bf%d_2" % a, [P, 2 * KP], BF16, tag="bf%d" % a) for a in range(k_passes)]
        for a in range(k_passes):
            interleave(second[:, KP * a : KP * (a + 1)], load_w1(a, raws[a], P, 2 * P))
        held["idx3"] = load_list("idx3", offs3)
        for a in range(k_passes):
            interleave(others[a][:], load_w1(a, raws[a], 2 * P, KP))
        for i in range(tiles):
            b, t = divmod(i, PACK)
            if i > 0:
                put_features(i, h, 0, S)
            if i == 0:
                codes = sbuf("w1_c_1", [P, k_passes * P], U32)
                for a in range(k_passes):
                    quantize_w1(a, 1, 2, second[:, KP * a : KP * (a + 1)], codes[:, P * a : P * (a + 1)])
                got = sbuf("got0", [P, S], F32, tag="second")
                recall(0, 0, got[:], 0, S)
            if i == PACK + 1:
                first = sbuf("x_c00", [P, QW], U32, tag="wgs_dealt0")
                quantize_x(0, 0, first[:], x_bf0[:, 0 : PACK * QW])
            if i + 1 < tiles:
                h = make_features(i + 1)
            if i == 0:
                gain_plain = sbuf("gain_plain", [P, PACK], F32)
                with nc.allow_non_contiguous_dma(reason="one gain for each partition"):
                    nc.sync.dma_start(gain_plain[:], gain[0:KP].rearrange("(c p) -> p c", p=P))
                held["gain_dealt"] = sbuf("gain_dealt", [P, PACK], F32)
                nc.sync.dma_start(held["gain_dealt"][:], gain[KP:].rearrange("(p t) -> p t", t=PACK))
                codes = sbuf("w1_c_2", [P, k_passes * 2 * P], U32, tag="row1")
                for a in range(k_passes):
                    quantize_w1(a, 2, PACK, others[a][:], codes[:, 2 * P * a : 2 * P * (a + 1)])
            else:
                got = sbuf("got%d" % i, [P, S], F32, tag="row%d" % ((i + 1) % 3))
            if b == 0:
                if i > 0:
                    recall(0, t, got[:], 0, S)
                rows = sbuf("scaled%d" % i, [P, S], BF16, tag=("scaled", "second", "page0", "page1")[i])
                nc.scalar.activation(rows[:], got[:], ACT.Copy, scale=gain_plain[:, i : i + 1])
                scaled.append(rows)
            else:
                if t < PACK - 1:
                    recall(1, t, got[:, 0 : early * QW], 0, early * QW)
                for q in range(early):
                    cols = slice(QW * q, QW * (q + 1))
                    if t == PACK - 1:
                        recall(1, t, got[:, cols], cols.start, cols.stop)
                    weave(1, t, x_bf1[q][:], got[:, cols])
            if i == 1:
                w1_bf = []
                for a in range(k_passes):
                    raw = sbuf("w1_raw%d_4" % a, [P, PACK * KP], F32, tag="raw%d" % a)
                    planes = load_w1(a, raw, KP, H)
                    woven = sbuf("w1_bf%d_4" % a, [P, PACK * KP], BF16, tag="bf%d" % a)
                    nc.scalar.copy(
                        woven[:].rearrange("p (t m i) -> p m t i", t=PACK, i=PACK),
                        planes.rearrange("p i (m t) -> p m t i", t=PACK),
                    )
                    w1_bf.append(woven)
            if i == 2:
                codes = sbuf("w1_c1", [P, k_passes * KP], U32, tag="page2")
                for a in range(k_passes):
                    quantize_w1(a, PACK, tiles, w1_bf[a][:], codes[:, KP * a : KP * (a + 1)])
                w3_bf = [round_w3(a) for a in range(r_passes)]
                x_bf1 = [sbuf("x_bf1%d" % q, [P, PACK * QW], BF16, tag="raw%d" % q) for q in range(early)]
            if i == 3:
                codes = sbuf("w3_c", [P, r_passes * N], U32, tag="page3")
                w3_q = [quantize_w3(a, w3_bf[a], codes[:, N * a : N * (a + 1)]) for a in range(r_passes)]
                w2_w = sbuf("w2_w", [P, r_passes, 2 * N], U8)
                nc.sync.dma_start(w2_w[:].bitcast(I32), w2_words.rearrange("a p c -> p a c").bitcast(I32))
                for quad in range(4):
                    nc.sync.dma_start(
                        w2_s[32 * quad : 32 * quad + 4, :, :].bitcast(I32),
                        w2_scales[:, 4 * quad : 4 * quad + 4, :].rearrange("a r c -> r a c").bitcast(I32),
                    )
            if i == 4:
                idx4 = load_list("idx4", offs4)
                wgo_sb = sbuf("wgo_sb", [P, S], F32)
                nc.sync.dma_start(wgo_sb[:], wgo)
                legible = []
                for n in range(n_tiles):
                    tile = sbuf("legible%d" % n, [P, T], F32, tag="wide%d" % n)
                    nc.sync.dma_start(tile[:], page1[P * n : P * (n + 1), :])
                    legible.append(tile)
                for c in range(PACK):
                    for plane in range(PACK):
                        nc.sync.dma_start(x_planes[32 * c : 32 * (c + 1), plane, :], scaled[c][plane:P:PACK, :])
                for q in range(QUARTERS):
                    interleave(x_bf0[:, PACK * QW * q : PACK * QW * (q + 1)], x_planes[:, :, QW * q : QW * (q + 1)])

        x_c0 = sbuf("x_c0", [P, early, QW], U32, tag="wgs_dealt1")

        def quantize_quarter(b, q):
            if b == 0:
                quantize_x(0, q, x_c0[:, q - 1, :], x_bf0[:, PACK * QW * q : PACK * QW * (q + 1)])
            else:
                codes = sbuf("x_c1%d" % q, [P, QW], U32)
                quantize_x(1, q, codes[:], x_bf1[q][:])

        quantize_quarter(1, 0)
        quantize_quarter(0, 1)
        quantize_quarter(1, 1)
        late = sbuf("late", [P, PACK, QW], F32, tag="raw0")
        for t in range(PACK):
            recall(1, t, late[:, t, :], early * QW, S)
        quantize_quarter(0, 2)
        quantize_quarter(1, 2)
        quantize_quarter(0, 3)

        square_tag = ["bf0", "bf1", "bf2", "bf0", "bf1", "bf2", "bf1", "bf2"]
        y_last = sbuf("y_last", [P, 2 * QW], F32)

        def score(q):
            accs = {}
            for jt in range(2):
                accs[jt] = (bank("y2_%d%d" % (q, jt), 2 * jt, N), bank("y3_%d%d" % (q, jt), 2 * jt + 1, N))
            for b in range(r_passes):
                codes, scales = x_q[b, q]
                for jt in range(2):
                    lhs = codes[:, P * jt : P * (jt + 1)].bitcast(FP8X4)
                    lhs_scale = scales[:, P * jt : P * (jt + 1)]
                    for n in range(n_tiles):
                        nc.tensor.matmul_mx(
                            out=accs[jt][0][:, P * n : P * (n + 1)],
                            lhsT=lhs,
                            lhsT_scale=lhs_scale,
                            rhs=w2_w[:, b, 2 * P * n : 2 * P * (n + 1)].bitcast(FP4X4),
                            rhs_scale=w2_s[:, b, P * n : P * (n + 1)],
                            start=(b == 0 and n == 0),
                            stop=(b == r_passes - 1 and n == n_tiles - 1),
                        )
                    for c0, c1 in ((0, 256), (256, N)):
                        nc.tensor.matmul_mx(
                            out=accs[jt][1][:, c0:c1],
                            lhsT=lhs,
                            lhsT_scale=lhs_scale,
                            rhs=w3_q[b][0][:, c0:c1].bitcast(FP8X4),
                            rhs_scale=w3_q[b][1][:, c0:c1],
                            start=(b == 0 and c0 == 0),
                            stop=(b == r_passes - 1 and c1 == N),
                        )
            sums = [bank("sum%d%d" % (q, n), 4 + (n_tiles * q + n) % 4, QW) for n in range(n_tiles)]
            for jt in range(2):
                squares = sbuf("sq%d%d" % (q, jt), [P, 2, N], F32, tag=square_tag[2 * q + jt])
                for which in range(2):
                    nc.scalar.activation(squares[:, which, :], accs[jt][which][:], ACT.Square)
                for n in range(n_tiles):
                    for which in range(2):
                        nc.tensor.matmul(
                            sums[n][:, P * jt : P * (jt + 1)],
                            squares[:, which, P * n : P * (n + 1)],
                            ident[:],
                            start=(which == 0),
                            stop=(which == 1),
                            is_transpose=True,
                        )
            for n in range(n_tiles):
                j0, j1 = QW * q, QW * (q + 1)
                joined = n == n_tiles - 1 and q >= QUARTERS - 2
                if joined:
                    y = y_last[:, QW * (q - 2) : QW * (q - 1)]
                else:
                    y_tile = sbuf("y%d%d" % (q, n), [P, QW], F32, tag="y", bufs=4)
                    y = y_tile[:]
                nc.scalar.activation(y, sums[n][:], ACT.Sqrt, bias=1.0)
                if joined:
                    if q == QUARTERS - 2:
                        continue
                    y, j0 = y_last[:], j0 - QW
                nc.vector.tensor_tensor(legible[n][:].indirect(entries(idx4, j0, j1)), y, wgo_sb[:, j0:j1], MULT)
                if q == QUARTERS - 1:
                    nc.sync.dma_start(out[P * n : P * (n + 1), :], legible[n][:])

        score(0)
        score(1)
        x_bf1.append(sbuf("x_bf13", [P, PACK * QW], BF16, tag="bf0"))
        late_bf = sbuf("late_bf", [P, PACK, QW], BF16, tag="scaled")
        for t in range(PACK):
            nc.scalar.activation(late_bf[:, t, :], late[:, t, :], ACT.Copy, scale=held["gain_dealt"][:, t : t + 1])
        interleave(x_bf1[early][:], late_bf[:])
        quantize_quarter(1, early)
        score(2)
        score(3)
